import numpy as np, ml_dtypes
CORES = [242,247,114,119]
N = 4
F = 256
def setup_inputs(rng):
    m = (rng.standard_normal((N, 128, 128), dtype=np.float32) / 11).astype(ml_dtypes.bfloat16)
    return {"m": m, "mt": m.transpose(0, 2, 1).copy(), "x": rng.standard_normal((N, 128, F), dtype=np.float32).astype(ml_dtypes.bfloat16)}
def setup_inputs_big(rng):
    d = setup_inputs(rng)
    for k in ("x",): d[k] = (d[k].astype(np.float32) * 1048576.0).astype(d[k].dtype)
    return d
def setup_inputs_small(rng):
    d = setup_inputs(rng)
    for k in ("x",): d[k] = (d[k].astype(np.float32) * (1 / 1048576.0)).astype(d[k].dtype)
    return d
def setup_inputs_apart(rng):
    d = setup_inputs(rng)
    f = (10.0 ** rng.permutation(np.linspace(-1.5, 1.5, N))).astype(np.float32).reshape(N, 1, 1)
    for k in ("x",): d[k] = (d[k].astype(np.float32) * f).astype(d[k].dtype)
    return d
def reference(m, mt, x):
    M, X = m.astype(np.float64), x.astype(np.float64)
    y = np.zeros((N, 128, F)); p = X[0]
    for r in range(N):
        p = M[r].T @ p
        y[r] = p
    return {"y": y.astype(ml_dtypes.bfloat16)}

@@ -1,0 +1,137 @@
+from concourse.bass import DstId, RemoteDMATransfer
+
+F = 256
+K = 128
+
+SCRATCH = {
+    "xs":   ("sbuf", [128, F], "bfloat16"),
+    "ms":   ("sbuf", [128, K], "bfloat16"),
+    "mts":  ("sbuf", [128, K], "bfloat16"),
+    "p0l":  ("sbuf", [128, F], "bfloat16"),
+    "mt1l": ("sbuf", [128, K], "bfloat16"),
+    "mt2l": ("sbuf", [128, K], "bfloat16"),
+    "bs":   ("sbuf", [128, K], "bfloat16"),
+    "rs":   ("sbuf", [128, K], "bfloat16"),
+    "ys":   ("sbuf", [128, F], "bfloat16"),
+    "psb":  ("psum", [128, 512], "float32"),
+    "psr":  ("psum", [128, 512], "float32"),
+    "psy":  ("psum", [128, 512], "float32"),
+}
+SEMAPHORES = ["ld_a", "ld_b", "a_p", "a_m1", "a_m2", "mm", "cp", "sent", "st"]
+
+
+def _engines(mask):
+    return [e for e in range(mask.bit_length()) if (mask >> e) & 1]
+
+
+def _bits(es):
+    b = 0
+    for e in es:
+        b |= 1 << e
+    return b
+
+
+def _deal(core, dsts, topo):
+    allowed = {d: _engines(topo.mask(core, d)) for d in dsts}
+    narrow = min(len(a) for a in allowed.values())
+    far = [d for d in dsts if len(allowed[d]) == narrow]
+    near = [d for d in dsts if len(allowed[d]) > narrow]
+    out = {}
+    pool = allowed[far[0]]
+    n = len(pool) // len(far)
+    while 128 % n:
+        n -= 1
+    for i, d in enumerate(far):
+        out[d] = _bits(pool[i * n:(i + 1) * n])
+    for d in near:
+        rest = [e for e in allowed[d] if e not in pool]
+        m = len(rest) // len(near)
+        while 128 % m:
+            m -= 1
+        j = near.index(d)
+        out[d] = _bits(rest[j * m:(j + 1) * m])
+    return out
+
+
+def _count(mask):
+    return len(_engines(mask))
+
+
+def _send(g, core, topo, src, dst_buf, dsts, remote_sem, local_sem):
+    masks = _deal(core, dsts, topo)
+    trs = []
+    for d in dsts:
+        rid, pid = topo.addr(d, core)
+        trs.append(RemoteDMATransfer(dst_ids=[DstId(rid=rid, pnc=pid)], dma_engine_mask=masks[d],
+                                     remote_sem=remote_sem, src=src, dst=dst_buf))
+    g.remote_dma_fused(trs, local_sem=local_sem)
+    return sum(_count(m) for m in masks.values())
+
+
+def rank_program(g, core, T, topo):
+    rank = T.rank_of(core)
+    if rank is None:
+        return
+    S = T.sem
+    C = T.cores
+    n_p = {d: _count(m) for d, m in _deal(C[0], [C[1], C[2], C[3]], topo).items()}
+    n_m1 = {d: _count(m) for d, m in _deal(C[1], [C[2], C[3]], topo).items()}
+    n_m2 = {d: _count(m) for d, m in _deal(C[2], [C[3]], topo).items()}
+    stage = [0]
+
+    def product(ps, lhsT, rhs, out):
+        stage[0] += 1
+        g.tensor.matmul(ps, lhsT, rhs, True, True).then_inc(S.mm, 1)
+        g.vector.wait_ge(S.mm, stage[0])
+        g.vector.tensor_copy(out, ps).then_inc(S.cp, 1)
+        return stage[0]
+
+    if rank == 0:
+        g.sync.dma_start(T.xs[:], T.x[:]).then_inc(S.ld_a, 16)
+        g.scalar.dma_start(T.ms[:], T.m[:]).then_inc(S.ld_b, 16)
+        g.tensor.wait_ge(S.ld_b, 16)
+        g.tensor.wait_ge(S.ld_a, 16)
+        k = product(T.psy[:, 0:F], T.ms[:], T.xs[:], T.ys[:])
+        g.wait_ge(S.cp, k)
+        tot = _send(g, core, topo, T.ys[:], T.p0l[:], [C[1], C[2], C[3]], S.a_p, S.sent)
+        g.sync.wait_ge(S.cp, k)
+        g.sync.wait_ge(S.sent, tot)
+        g.sync.dma_start(T.y[:], T.ys[:]).then_inc(S.st, 16)
+        g.sync.wait_ge(S.st, 16)
+        return
+
+    if rank == 1:
+        g.sync.dma_start(T.mts[:], T.mt[:]).then_inc(S.ld_a, 16)
+        g.scalar.dma_start(T.ms[:], T.m[:]).then_inc(S.ld_b, 16)
+        g.wait_ge(S.ld_a, 16)
+        tot = _send(g, core, topo, T.mts[:], T.mt1l[:], [C[2], C[3]], S.a_m1, S.sent)
+        g.wait_ge(S.sent, tot)
+        g.tensor.wait_ge(S.ld_b, 16)
+        lhs = T.ms
+    elif rank == 2:
+        g.sync.dma_start(T.mts[:], T.mt[:]).then_inc(S.ld_a, 16)
+        g.scalar.dma_start(T.ms[:], T.m[:]).then_inc(S.ld_b, 16)
+        g.wait_ge(S.ld_a, 16)
+        tot = _send(g, core, topo, T.mts[:], T.mt2l[:], [C[3]], S.a_m2, S.sent)
+        g.wait_ge(S.sent, tot)
+        g.tensor.wait_ge(S.ld_b, 16)
+        g.tensor.wait_ge(S.a_m1, n_m1[core])
+        k = product(T.psr[:, 0:K], T.mt1l[:], T.ms[:], T.rs[:])
+        g.tensor.wait_ge(S.cp, k)
+        lhs = T.rs
+    else:
+        g.sync.dma_start(T.ms[:], T.m[:]).then_inc(S.ld_b, 16)
+        g.tensor.wait_ge(S.ld_b, 16)
+        g.tensor.wait_ge(S.a_m2, n_m2[core])
+        k = product(T.psb[:, 0:K], T.mt2l[:], T.ms[:], T.bs[:])
+        g.tensor.wait_ge(S.cp, k)
+        g.tensor.wait_ge(S.a_m1, n_m1[core])
+        k = product(T.psr[:, 0:K], T.mt1l[:], T.bs[:], T.rs[:])
+        g.tensor.wait_ge(S.cp, k)
+        lhs = T.rs
+
+    g.tensor.wait_ge(S.a_p, n_p[core])
+    k = product(T.psy[:, 0:F], lhs[:], T.p0l[:], T.ys[:])
+    g.sync.wait_ge(S.cp, k)
+    g.sync.dma_start(T.y[:], T.ys[:]).then_inc(S.st, 16)
+    g.sync.wait_ge(S.st, 16)

@@ -4,7 +4,8 @@ F = 256
 K = 128
 
 SCRATCH = {
-    "xs":   ("sbuf", [128, F], "bfloat16"),
+    "xm":   ("sbuf", [128, F + K], "bfloat16"),
+    "xml":  ("sbuf", [128, F + K], "bfloat16"),
     "ms":   ("sbuf", [128, K], "bfloat16"),
     "mts":  ("sbuf", [128, K], "bfloat16"),
     "p0l":  ("sbuf", [128, F], "bfloat16"),
@@ -31,38 +32,26 @@ def _bits(es):
     return b
 
 
-def _deal(core, dsts, topo):
-    allowed = {d: _engines(topo.mask(core, d)) for d in dsts}
-    narrow = min(len(a) for a in allowed.values())
-    far = [d for d in dsts if len(allowed[d]) == narrow]
-    near = [d for d in dsts if len(allowed[d]) > narrow]
-    out = {}
-    pool = allowed[far[0]]
-    n = len(pool) // len(far)
-    while 128 % n:
-        n -= 1
-    for i, d in enumerate(far):
-        out[d] = _bits(pool[i * n:(i + 1) * n])
-    for d in near:
-        rest = [e for e in allowed[d] if e not in pool]
-        m = len(rest) // len(near)
-        while 128 % m:
-            m -= 1
-        j = near.index(d)
-        out[d] = _bits(rest[j * m:(j + 1) * m])
-    return out
-
-
 def _count(mask):
     return len(_engines(mask))
 
 
-def _send(g, core, topo, src, dst_buf, dsts, remote_sem, local_sem):
-    masks = _deal(core, dsts, topo)
-    trs = []
+def _deal(core, dsts, topo, keep_off=0):
+    common = ~keep_off
     for d in dsts:
+        common &= topo.mask(core, d)
+    pool = _engines(common)
+    n = len(pool) // len(dsts)
+    while 128 % n:
+        n -= 1
+    return {d: _bits(pool[i * n:(i + 1) * n]) for i, d in enumerate(dsts)}
+
+
+def _send(g, core, topo, src, dst_buf, masks, remote_sem, local_sem):
+    trs = []
+    for d, m in masks.items():
         rid, pid = topo.addr(d, core)
-        trs.append(RemoteDMATransfer(dst_ids=[DstId(rid=rid, pnc=pid)], dma_engine_mask=masks[d],
+        trs.append(RemoteDMATransfer(dst_ids=[DstId(rid=rid, pnc=pid)], dma_engine_mask=m,
                                      remote_sem=remote_sem, src=src, dst=dst_buf))
     g.remote_dma_fused(trs, local_sem=local_sem)
     return sum(_count(m) for m in masks.values())
@@ -74,9 +63,10 @@ def rank_program(g, core, T, topo):
         return
     S = T.sem
     C = T.cores
-    n_p = {d: _count(m) for d, m in _deal(C[0], [C[1], C[2], C[3]], topo).items()}
-    n_m1 = {d: _count(m) for d, m in _deal(C[1], [C[2], C[3]], topo).items()}
-    n_m2 = {d: _count(m) for d, m in _deal(C[2], [C[3]], topo).items()}
+    k_p = _deal(C[0], [C[2], C[3]], topo)
+    k_x = _deal(C[0], [C[1]], topo, keep_off=_bits(_engines(k_p[C[2]] | k_p[C[3]])))
+    k_m1 = _deal(C[1], [C[2], C[3]], topo)
+    k_m2 = _deal(C[2], [C[3]], topo)
     stage = [0]
 
     def product(ps, lhsT, rhs, out):
@@ -87,13 +77,16 @@ def rank_program(g, core, T, topo):
         return stage[0]
 
     if rank == 0:
-        g.sync.dma_start(T.xs[:], T.x[:]).then_inc(S.ld_a, 16)
-        g.scalar.dma_start(T.ms[:], T.m[:]).then_inc(S.ld_b, 16)
+        g.sync.dma_start(T.xm[:, 0:F], T.x[:]).then_inc(S.ld_a, 16)
+        g.scalar.dma_start(T.xm[:, F:F + K], T.m[:]).then_inc(S.ld_b, 16)
         g.tensor.wait_ge(S.ld_b, 16)
         g.tensor.wait_ge(S.ld_a, 16)
-        k = product(T.psy[:, 0:F], T.ms[:], T.xs[:], T.ys[:])
+        k = product(T.psy[:, 0:F], T.xm[:, F:F + K], T.xm[:, 0:F], T.ys[:])
+        g.wait_ge(S.ld_b, 16)
+        g.wait_ge(S.ld_a, 16)
+        tot = _send(g, core, topo, T.xm[:], T.xml[:], k_x, S.a_p, S.sent)
         g.wait_ge(S.cp, k)
-        tot = _send(g, core, topo, T.ys[:], T.p0l[:], [C[1], C[2], C[3]], S.a_p, S.sent)
+        tot += _send(g, core, topo, T.ys[:], T.p0l[:], k_p, S.a_p, S.sent)
         g.sync.wait_ge(S.cp, k)
         g.sync.wait_ge(S.sent, tot)
         g.sync.dma_start(T.y[:], T.ys[:]).then_inc(S.st, 16)
@@ -104,33 +97,37 @@ def rank_program(g, core, T, topo):
         g.sync.dma_start(T.mts[:], T.mt[:]).then_inc(S.ld_a, 16)
         g.scalar.dma_start(T.ms[:], T.m[:]).then_inc(S.ld_b, 16)
         g.wait_ge(S.ld_a, 16)
-        tot = _send(g, core, topo, T.mts[:], T.mt1l[:], [C[2], C[3]], S.a_m1, S.sent)
+        tot = _send(g, core, topo, T.mts[:], T.mt1l[:], k_m1, S.a_m1, S.sent)
         g.wait_ge(S.sent, tot)
         g.tensor.wait_ge(S.ld_b, 16)
+        g.tensor.wait_ge(S.a_p, _count(k_x[core]))
+        k = product(T.psr[:, 0:F], T.xml[:, F:F + K], T.xml[:, 0:F], T.p0l[:])
+        g.tensor.wait_ge(S.cp, k)
         lhs = T.ms
     elif rank == 2:
         g.sync.dma_start(T.mts[:], T.mt[:]).then_inc(S.ld_a, 16)
         g.scalar.dma_start(T.ms[:], T.m[:]).then_inc(S.ld_b, 16)
         g.wait_ge(S.ld_a, 16)
-        tot = _send(g, core, topo, T.mts[:], T.mt2l[:], [C[3]], S.a_m2, S.sent)
+        tot = _send(g, core, topo, T.mts[:], T.mt2l[:], k_m2, S.a_m2, S.sent)
         g.wait_ge(S.sent, tot)
         g.tensor.wait_ge(S.ld_b, 16)
-        g.tensor.wait_ge(S.a_m1, n_m1[core])
+        g.tensor.wait_ge(S.a_m1, _count(k_m1[core]))
         k = product(T.psr[:, 0:K], T.mt1l[:], T.ms[:], T.rs[:])
         g.tensor.wait_ge(S.cp, k)
+        g.tensor.wait_ge(S.a_p, _count(k_p[core]))
         lhs = T.rs
     else:
         g.sync.dma_start(T.ms[:], T.m[:]).then_inc(S.ld_b, 16)
         g.tensor.wait_ge(S.ld_b, 16)
-        g.tensor.wait_ge(S.a_m2, n_m2[core])
+        g.tensor.wait_ge(S.a_m2, _count(k_m2[core]))
         k = product(T.psb[:, 0:K], T.mt2l[:], T.ms[:], T.bs[:])
         g.tensor.wait_ge(S.cp, k)
-        g.tensor.wait_ge(S.a_m1, n_m1[core])
+        g.tensor.wait_ge(S.a_m1, _count(k_m1[core]))
         k = product(T.psr[:, 0:K], T.mt1l[:], T.bs[:], T.rs[:])
         g.tensor.wait_ge(S.cp, k)
+        g.tensor.wait_ge(S.a_p, _count(k_p[core]))
         lhs = T.rs
 
-    g.tensor.wait_ge(S.a_p, n_p[core])
     k = product(T.psy[:, 0:F], lhs[:], T.p0l[:], T.ys[:])
     g.sync.wait_ge(S.cp, k)
     g.sync.dma_start(T.y[:], T.ys[:]).then_inc(S.st, 16)

from concourse.bass import DstId, RemoteDMATransfer

F = 256
K = 128

SCRATCH = {
    "xm":   ("sbuf", [128, F + K], "bfloat16"),
    "xml":  ("sbuf", [128, F + K], "bfloat16"),
    "ms":   ("sbuf", [128, K], "bfloat16"),
    "mts":  ("sbuf", [128, K], "bfloat16"),
    "p0l":  ("sbuf", [128, F], "bfloat16"),
    "mt1l": ("sbuf", [128, K], "bfloat16"),
    "mt2l": ("sbuf", [128, K], "bfloat16"),
    "bs":   ("sbuf", [128, K], "bfloat16"),
    "rs":   ("sbuf", [128, K], "bfloat16"),
    "ys":   ("sbuf", [128, F], "bfloat16"),
    "psb":  ("psum", [128, 512], "float32"),
    "psr":  ("psum", [128, 512], "float32"),
    "psy":  ("psum", [128, 512], "float32"),
}
SEMAPHORES = ["ld_a", "ld_b", "a_p", "a_m1", "a_m2", "mm", "cp", "sent", "st"]


def _engines(mask):
    return [e for e in range(mask.bit_length()) if (mask >> e) & 1]


def _bits(es):
    b = 0
    for e in es:
        b |= 1 << e
    return b


def _count(mask):
    return len(_engines(mask))


def _deal(core, dsts, topo, keep_off=0):
    common = ~keep_off
    for d in dsts:
        common &= topo.mask(core, d)
    pool = _engines(common)
    n = len(pool) // len(dsts)
    while 128 % n:
        n -= 1
    return {d: _bits(pool[i * n:(i + 1) * n]) for i, d in enumerate(dsts)}


def _send(g, core, topo, src, dst_buf, masks, remote_sem, local_sem):
    trs = []
    for d, m in masks.items():
        rid, pid = topo.addr(d, core)
        trs.append(RemoteDMATransfer(dst_ids=[DstId(rid=rid, pnc=pid)], dma_engine_mask=m,
                                     remote_sem=remote_sem, src=src, dst=dst_buf))
    g.remote_dma_fused(trs, local_sem=local_sem)
    return sum(_count(m) for m in masks.values())


def rank_program(g, core, T, topo):
    rank = T.rank_of(core)
    if rank is None:
        return
    S = T.sem
    C = T.cores
    k_p = _deal(C[0], [C[2], C[3]], topo)
    k_x = _deal(C[0], [C[1]], topo, keep_off=_bits(_engines(k_p[C[2]] | k_p[C[3]])))
    k_m1 = _deal(C[1], [C[2], C[3]], topo)
    k_m2 = _deal(C[2], [C[3]], topo)
    stage = [0]

    def product(ps, lhsT, rhs, out):
        stage[0] += 1
        g.tensor.matmul(ps, lhsT, rhs, True, True).then_inc(S.mm, 1)
        g.vector.wait_ge(S.mm, stage[0])
        g.vector.tensor_copy(out, ps).then_inc(S.cp, 1)
        return stage[0]

    if rank == 0:
        g.sync.dma_start(T.xm[:, 0:F], T.x[:]).then_inc(S.ld_a, 16)
        g.scalar.dma_start(T.xm[:, F:F + K], T.m[:]).then_inc(S.ld_b, 16)
        g.tensor.wait_ge(S.ld_b, 16)
        g.tensor.wait_ge(S.ld_a, 16)
        k = product(T.psy[:, 0:F], T.xm[:, F:F + K], T.xm[:, 0:F], T.ys[:])
        g.wait_ge(S.ld_b, 16)
        g.wait_ge(S.ld_a, 16)
        tot = _send(g, core, topo, T.xm[:], T.xml[:], k_x, S.a_p, S.sent)
        g.wait_ge(S.cp, k)
        tot += _send(g, core, topo, T.ys[:], T.p0l[:], k_p, S.a_p, S.sent)
        g.sync.wait_ge(S.cp, k)
        g.sync.wait_ge(S.sent, tot)
        g.sync.dma_start(T.y[:], T.ys[:]).then_inc(S.st, 16)
        g.sync.wait_ge(S.st, 16)
        return

    if rank == 1:
        g.sync.dma_start(T.mts[:], T.mt[:]).then_inc(S.ld_a, 16)
        g.scalar.dma_start(T.ms[:], T.m[:]).then_inc(S.ld_b, 16)
        g.wait_ge(S.ld_a, 16)
        tot = _send(g, core, topo, T.mts[:], T.mt1l[:], k_m1, S.a_m1, S.sent)
        g.wait_ge(S.sent, tot)
        g.tensor.wait_ge(S.ld_b, 16)
        g.tensor.wait_ge(S.a_p, _count(k_x[core]))
        k = product(T.psr[:, 0:F], T.xml[:, F:F + K], T.xml[:, 0:F], T.p0l[:])
        g.tensor.wait_ge(S.cp, k)
        lhs = T.ms
    elif rank == 2:
        g.sync.dma_start(T.mts[:], T.mt[:]).then_inc(S.ld_a, 16)
        g.scalar.dma_start(T.ms[:], T.m[:]).then_inc(S.ld_b, 16)
        g.wait_ge(S.ld_a, 16)
        tot = _send(g, core, topo, T.mts[:], T.mt2l[:], k_m2, S.a_m2, S.sent)
        g.wait_ge(S.sent, tot)
        g.tensor.wait_ge(S.ld_b, 16)
        g.tensor.wait_ge(S.a_m1, _count(k_m1[core]))
        k = product(T.psr[:, 0:K], T.mt1l[:], T.ms[:], T.rs[:])
        g.tensor.wait_ge(S.cp, k)
        g.tensor.wait_ge(S.a_p, _count(k_p[core]))
        lhs = T.rs
    else:
        g.sync.dma_start(T.ms[:], T.m[:]).then_inc(S.ld_b, 16)
        g.tensor.wait_ge(S.ld_b, 16)
        g.tensor.wait_ge(S.a_m2, _count(k_m2[core]))
        k = product(T.psb[:, 0:K], T.mt2l[:], T.ms[:], T.bs[:])
        g.tensor.wait_ge(S.cp, k)
        g.tensor.wait_ge(S.a_m1, _count(k_m1[core]))
        k = product(T.psr[:, 0:K], T.mt1l[:], T.bs[:], T.rs[:])
        g.tensor.wait_ge(S.cp, k)
        g.tensor.wait_ge(S.a_p, _count(k_p[core]))
        lhs = T.rs

    k = product(T.psy[:, 0:F], lhs[:], T.p0l[:], T.ys[:])
    g.sync.wait_ge(S.cp, k)
    g.sync.dma_start(T.y[:], T.ys[:]).then_inc(S.st, 16)
    g.sync.wait_ge(S.st, 16)
